import numpy as np
import ml_dtypes


def mxq(x, axis, fmt="e4m3"):
    dtype, down = {"e4m3": (ml_dtypes.float8_e4m3fn, 7), "e5m2": (ml_dtypes.float8_e5m2, 14)}[fmt]
    v = np.moveaxis(np.asarray(x, np.float32).astype(ml_dtypes.bfloat16).astype(np.float64), axis, -1)
    blocks = v.reshape(v.shape[:-1] + (-1, 32))
    amax = np.abs(blocks).max(-1, keepdims=True)
    byte = np.maximum(np.where(amax > 0, np.frexp(amax)[1] - 1 + 127, 0) - down, 1)
    scale = np.exp2(byte - 127.0)
    codes = (blocks / scale).astype(np.float32).astype(dtype).astype(np.float64)
    return np.moveaxis((codes * scale).reshape(v.shape), -1, axis)


WIDE = False


def mx_kscale(k):
    if not WIDE:
        return np.ones(k)
    levels = np.array([10, -10, 5, -5, 0])
    if k % 512:
        return np.exp2(np.random.permutation(np.resize(levels, k // 32))).repeat(32)
    a = np.empty((k // 512, 16))
    for p in range(k // 512):
        a[p, :8] = np.random.permutation(np.resize(levels, 8))
        for g in range(8):
            far = levels[np.abs(levels - a[p, g]) >= 10]
            a[p, g + 8] = far[np.random.randint(len(far))]
    return np.exp2(a.ravel()).repeat(32)


def f64(x):
    return np.asarray(x).astype(np.float64)


def striped(idx):
    return np.tile(idx.reshape(-1, 16).T, (8, 1)).astype(np.uint16)


def unstriped(offs):
    return offs[:16].T.reshape(-1).astype(np.int64)


def striped8(idx):
    return np.concatenate([x.reshape(-1, 16).T for x in idx]).astype(np.uint16)


def runs(offs, k):
    lists = np.stack([offs[16 * r : 16 * r + 16].T.reshape(-1) for r in range(8)]).astype(np.int64)
    return lists[np.arange(k) % 512 // 64]


def pack_weight(w):
    k, n = w.shape
    w = f64(np.asarray(w, np.float32).astype(ml_dtypes.bfloat16)).reshape(k // 32, 32, n)
    amax = np.abs(w).max(1)
    byte = np.clip(np.where(amax > 0, np.frexp(amax)[1] - 1 + 127 - 7, 1), 1, 254)
    scaled = (w * np.exp2(127.0 - byte)[:, None, :]).reshape(k, n).astype(np.float32)
    words = np.ascontiguousarray(scaled.reshape(k // 512, 128, 4, n).transpose(0, 1, 3, 2)).astype(ml_dtypes.float8_e4m3fn).view(np.uint8)
    return words, np.ascontiguousarray(byte.astype(np.uint8).reshape(k // 512, 16, n))


def unpack_weight(words, scales):
    g, p, n, _ = words.shape
    vals = np.ascontiguousarray(words).view(ml_dtypes.float8_e4m3fn).astype(np.float64) * np.repeat(np.exp2(scales.astype(np.float64) - 127.0), 8, axis=1)[..., None]
    return vals.transpose(0, 1, 3, 2).reshape(g * 512, n)

def planes(y):
    n, m = y.shape
    v = y.astype(np.float32).astype(ml_dtypes.bfloat16).astype(np.float64).reshape(n // 32, 32, m)
    top = np.abs(v).max(1)
    byte = np.clip(np.where(top > 0, np.frexp(top)[1] - 1 + 127 - 7, 1), 1, 254)
    codes = (v * np.exp2(127.0 - byte)[:, None, :]).reshape(n, m).astype(np.float32).astype(ml_dtypes.float8_e4m3fn).view(np.uint8)
    words = codes.reshape(n // 512, 128, 4, m).transpose(0, 1, 3, 2)
    return np.ascontiguousarray(words), np.ascontiguousarray(byte.astype(np.uint8).reshape(n // 512, 16, m))


K, T, S, N, H = 512, 2048, 512, 512, 512


def setup_inputs():
    n = np.random.standard_normal
    s = mx_kscale(K)[:, None]
    u = mx_kscale(H)
    packed_xT = pack_weight(n((K, T)) * s)
    packed_w1 = pack_weight(n((K, H)) / np.sqrt(K) / s)
    packed_w2 = pack_weight(n((H, N)) / np.sqrt(H) / u[:, None])
    return {
        "x_words": packed_xT[0],
        "x_scales": packed_xT[1],
        "w1_words": packed_w1[0],
        "w1_scales": packed_w1[1],
        "gn": (np.random.uniform(0.5, 1.5, (H, 1)) * u[:, None]).astype(np.float32),
        "w2_words": packed_w2[0],
        "w2_scales": packed_w2[1],
        "offs": striped(np.random.permutation(T)[:S]),
        "n1": striped8(np.stack([np.random.permutation(S) for _ in range(8)])),
        "n2": striped8(np.stack([np.random.permutation(S) for _ in range(8)])),
        "n3": striped8(np.stack([np.random.permutation(S) for _ in range(8)])),
    }


def reference(x_words, x_scales, w1_words, w1_scales, gn, w2_words, w2_scales, offs, n1, n2, n3):
    xq = unpack_weight(x_words, x_scales)[:, unstriped(offs)]
    y = unpack_weight(w1_words, w1_scales).T @ xq
    z = f64(gn) * (np.exp(-1.0 * (np.abs(y[np.arange(H)[:, None], runs(n1, H)] - (y[np.arange(H)[:, None], runs(n2, H)])))))
    h = unpack_weight(w2_words, w2_scales).T @ mxq(z, 0, "e4m3")
    a = h[np.arange(N)[:, None], runs(n3, N)]
    out_0 = (h * a) / ((a) ** 2 + 0.5)
    return (out_0,) + planes(out_0)

@@ -1,0 +1,227 @@
+from contextlib import ExitStack
+
+import concourse.mybir as mybir
+
+K, T, S, H, N = 512, 2048, 512, 512, 512
+FLOPS = 2 * K * H * S + 2 * H * N * S
+
+F32 = mybir.dt.float32
+BF16 = mybir.dt.bfloat16
+I32 = mybir.dt.int32
+U32 = mybir.dt.uint32
+U16 = mybir.dt.uint16
+U8 = mybir.dt.uint8
+FP8X4 = mybir.dt.float8_e4m3fn_x4
+ACT = mybir.ActivationFunctionType
+ALU = mybir.AluOpType
+
+P = 128
+PACK = 4
+BANK = 512
+HALF = S // 2
+
+
+def half(c):
+    return slice(c * HALF, (c + 1) * HALF)
+
+
+def entries(lst, c):
+    return lst[:, c * HALF // 16 : (c + 1) * HALF // 16]
+
+
+def product(nc, out, words, scales, t, rhs, rhs_scale):
+    cols = slice(t * P, (t + 1) * P)
+    nc.tensor.matmul_mx(
+        out=out,
+        lhsT=words[:, cols].bitcast(FP8X4),
+        lhsT_scale=scales[:, cols],
+        rhs=rhs.bitcast(FP8X4),
+        rhs_scale=rhs_scale,
+        start=True,
+        stop=True,
+    )
+
+
+def load_scale_rows(queues, plane, scales):
+    for q, queue in enumerate(queues):
+        queue.dma_start(out=plane[32 * q : 32 * q + 4, :].bitcast(I32), in_=scales[0, 4 * q : 4 * q + 4, :].bitcast(I32))
+
+
+def deal(nc, out, in_, run):
+    nc.vector.tensor_copy(
+        out=out.rearrange("p (t c i) -> p c t i", t=PACK, i=run),
+        in_=in_.rearrange("p (c i t) -> p c t i", t=PACK, i=run),
+    )
+
+
+def tile_picked_laplace8_none_po_kernel(
+    tc, x_words, x_scales, w1_words, w1_scales, gn, w2_words, w2_scales, offs, n1, n2, n3, out_0, out_1, out_2
+):
+    nc = tc.nc
+    with ExitStack() as ctx:
+        lists = ctx.enter_context(tc.tile_pool(name="lists", bufs=1))
+        sb = ctx.enter_context(tc.tile_pool(name="sb", bufs=1))
+        psum = ctx.enter_context(tc.psum_pool(name="psum", bufs=1))
+
+        offs_t = lists.tile([P, S // 16], U16, name="offs_t")
+        n1_t = lists.tile([P, S // 16], U16, name="n1_t")
+        n2_t = lists.tile([P, S // 16], U16, name="n2_t")
+        n3_t = lists.tile([P, S // 16], U16, name="n3_t")
+
+        xw = sb.tile([P, T], I32, name="xw", align_bytes=64)
+        xs = sb.tile([P, T], U8, name="xs", align_bytes=64)
+        w1w = sb.tile([P, H], I32, name="w1w", tag="wraw", align_bytes=64)
+        ws = sb.tile([P, H], U8, name="ws", align_bytes=64)
+        gain = sb.tile([P, PACK], F32, name="gain")
+
+        nc.vector.memset(xs[:].bitcast(I32), 0)
+        nc.gpsimd.memset(ws[:].bitcast(I32), 0)
+
+        load_scale_rows([nc.scalar] * 4, xs, x_scales)
+        load_scale_rows([nc.scalar, nc.scalar, nc.scalar, nc.gpsimd], ws, w1_scales)
+        nc.sync.dma_start(offs_t[:], offs)
+        nc.sync.dma_start(n1_t[:], n1)
+        nc.sync.dma_start(n2_t[:], n2)
+        nc.sync.dma_start(n3_t[:], n3)
+        nc.sync.dma_start(out=w1w[:], in_=w1_words[0].rearrange("p n t -> p (n t)").bitcast(I32))
+        nc.sync.dma_start(out=xw[:], in_=x_words[0].rearrange("p n t -> p (n t)").bitcast(I32))
+        nc.gpsimd.dma_start(out=gain[:], in_=gn.rearrange("(p t) o -> p (t o)", t=PACK))
+
+        w1d = sb.tile([P, H], I32, name="w1d", align_bytes=64)
+        w1sd = sb.tile([P, H], U8, name="w1sd", align_bytes=64)
+        deal(nc, w1d[:], w1w[:], 4)
+        w2w = sb.tile([P, N], I32, name="w2w", tag="wraw", align_bytes=64)
+        nc.sync.dma_start(out=w2w[:], in_=w2_words[0].rearrange("p n t -> p (n t)").bitcast(I32))
+        xsg = sb.tile([P, S], U8, name="xsg", align_bytes=64)
+        nc.vector.tensor_copy(xsg[:], xs[:].indirect(offs_t[:]))
+        deal(nc, w1sd[:], ws[:], 16)
+        load_scale_rows([nc.sync] * 4, ws, w2_scales)
+
+        y = [sb.tile([P, S], F32, name="y%d" % t) for t in range(PACK)]
+        acc1 = {}
+        for c in range(2):
+            xg = sb.tile([P, HALF], U32, name="xg%d" % c, align_bytes=64)
+            nc.vector.tensor_copy(xg[:], xw[:].bitcast(U32).indirect(entries(offs_t, c)))
+            for t in range(PACK):
+                acc1[c, t] = psum.tile([P, BANK], F32, name="acc", tag="bank%d" % (PACK * c + t))
+                product(nc, acc1[c, t][:, :HALF], w1d, w1sd, t, xg[:], xsg[:, half(c)])
+        for t in range(PACK):
+            for c in range(2):
+                nc.scalar.activation(y[t][:, half(c)], acc1[c, t][:, :HALF], ACT.Copy)
+
+        w2d = sb.tile([P, N], I32, name="w2d", align_bytes=64)
+        w2sd = sb.tile([P, N], U8, name="w2sd", align_bytes=64)
+        deal(nc, w2d[:], w2w[:], 4)
+
+        diff = [sb.tile([P, PACK, HALF], F32, name="diff%d" % c) for c in range(2)]
+        size = [sb.tile([P, PACK, HALF], F32, name="size%d" % c, tag="size%d" % c) for c in range(2)]
+        decay = [sb.tile([P, PACK, HALF], F32, name="decay%d" % c, tag="decay%d" % c, align_bytes=64) for c in range(2)]
+        hs = [sb.tile([P, PACK, HALF], F32, name="hs%d" % c) for c in range(2)]
+        sq = [sb.tile([P, PACK, HALF], F32, name="sq%d" % c) for c in range(2)]
+        first = {}
+        zb = {}
+        acc2 = {}
+
+        def fetch_first(c, t, tag):
+            first[c, t] = sb.tile([P, HALF], F32, name="first", tag=tag, align_bytes=64)
+            nc.vector.tensor_copy(first[c, t][:], y[t][:].indirect(entries(n1_t, c)))
+
+        def fetch_second(c, t):
+            nc.vector.tensor_tensor(diff[c][:, t, :], y[t][:].indirect(entries(n2_t, c)), first[c, t][:], ALU.subtract)
+            nc.scalar.activation(size[c][:, t, :], diff[c][:, t, :], ACT.Abs)
+            nc.scalar.activation(decay[c][:, t, :], size[c][:, t, :], ACT.Exp, scale=-1.0)
+
+        def apply_gain(c):
+            zb[c] = sb.tile([P, HALF, PACK], BF16, name="zb", tag="zb%d" % c, align_bytes=64)
+            nc.vector.tensor_tensor(
+                zb[c][:].rearrange("p (c i) t -> p c t i", i=4),
+                decay[c][:].rearrange("p t (c i) -> p c t i", i=4),
+                gain[:].unsqueeze(1).unsqueeze(3).broadcast_to([P, HALF // 4, PACK, 4]),
+                ALU.mult,
+            )
+
+        def second_product(c):
+            zw = sb.tile([P, HALF], U32, name="zw%d" % c, align_bytes=64)
+            zs = sb.tile([P, HALF], U8, name="zs%d" % c, align_bytes=64)
+            nc.vector.quantize_mx(out=zw[:].bitcast(FP8X4), scales=zs[:], in_=zb[c][:].rearrange("p j t -> p (j t)"))
+            for t in range(PACK):
+                acc2[c, t] = psum.tile([P, BANK], F32, name="acc", tag="bank%d" % (PACK * c + t))
+                product(nc, acc2[c, t][:, :HALF], w2d, w2sd, t, zw[:], zs[:])
+
+        def square_h(c, t):
+            nc.scalar.activation(sq[c][:, t, :], acc2[c, t][:, :HALF], ACT.Square)
+
+        def keep_h(c, t):
+            nc.vector.tensor_copy(hs[c][:, t, :], acc2[c, t][:, :HALF])
+
+        fetch_first(0, 0, "first00")
+        for t in range(PACK):
+            if t + 1 < PACK:
+                fetch_first(0, t + 1, "first0%d" % (t + 1))
+            else:
+                fetch_first(1, 0, "first10")
+            fetch_second(0, t)
+        fetch_second(1, 0)
+        deal(nc, w2sd[:], ws[:], 16)
+        apply_gain(0)
+        fetch_first(1, 1, "decay0")
+        second_product(0)
+        fetch_first(1, 2, "zb0")
+        fetch_second(1, 1)
+        for t in range(PACK):
+            square_h(0, t)
+        fetch_first(1, 3, "decay0")
+        fetch_second(1, 2)
+        fetch_second(1, 3)
+        apply_gain(1)
+        second_product(1)
+        for t in range(PACK):
+            keep_h(0, t)
+
+        g = [sb.tile([P, S], F32, name="g%d" % t) for t in range(PACK)]
+        root = [sb.tile([P, PACK, HALF], F32, name="root%d" % c, tag="size%d" % (1 - c)) for c in range(2)]
+        inv = [sb.tile([P, PACK, HALF], F32, name="inv%d" % c) for c in range(2)]
+        for t in range(PACK):
+            keep_h(1, t)
+            square_h(1, t)
+            for c in (1, 0):
+                nc.scalar.activation(root[c][:, t, :], sq[c][:, t, :], ACT.Abs_reciprocal_sqrt, bias=0.5)
+                nc.scalar.activation(inv[c][:, t, :], root[c][:, t, :], ACT.Square)
+                nc.vector.tensor_tensor(g[t][:, half(c)], inv[c][:, t, :], hs[c][:, t, :], ALU.mult)
+
+        out_rows = out_0.rearrange("(p t) j -> p t j", t=PACK)
+        out_words = out_1[0].rearrange("p n t -> p (n t)").bitcast(I32)
+        ow = sb.tile([P, S], U32, name="ow", align_bytes=64)
+        osc = sb.tile([P, S], U8, name="osc", align_bytes=64)
+        res = [sb.tile([P, PACK, HALF], F32, name="res%d" % c) for c in range(2)]
+
+        def fetch_third(c, t):
+            nc.vector.tensor_tensor(res[c][:, t, :], g[t][:].indirect(entries(n3_t, c)), hs[c][:, t, :], ALU.mult)
+
+        def store_rows(c, t0, t1):
+            nc.sync.dma_start(out=out_rows[:, t0:t1, half(c)], in_=res[c][:, t0:t1, :])
+
+        def planes(c, copy):
+            ob = sb.tile([P, HALF, PACK], BF16, name="ob%d" % c, align_bytes=64)
+            copy(ob[:].rearrange("p (c i) t -> p c t i", i=4), res[c][:].rearrange("p t (c i) -> p c t i", i=4))
+            nc.vector.quantize_mx(
+                out=ow[:, half(c)].bitcast(FP8X4), scales=osc[:, half(c)], in_=ob[:].rearrange("p j t -> p (j t)")
+            )
+            nc.sync.dma_start(out=out_words[:, half(c)], in_=ow[:, half(c)].bitcast(I32))
+
+        for t in range(2):
+            for c in range(2):
+                fetch_third(c, t)
+        for c in range(2):
+            store_rows(c, 0, 2)
+        fetch_third(0, 2)
+        fetch_third(0, 3)
+        store_rows(0, 2, 4)
+        fetch_third(1, 2)
+        store_rows(1, 2, 3)
+        fetch_third(1, 3)
+        store_rows(1, 3, 4)
+        planes(1, nc.vector.tensor_copy)
+        planes(0, nc.scalar.copy)
+        for q in range(4):
+            nc.scalar.dma_start(out=out_2[0, 4 * q : 4 * q + 4, :].bitcast(I32), in_=osc[32 * q : 32 * q + 4, :].bitcast(I32))

@@ -25,8 +25,8 @@ def half(c):
     return slice(c * HALF, (c + 1) * HALF)
 
 
-def entries(lst, c):
-    return lst[:, c * HALF // 16 : (c + 1) * HALF // 16]
+def entries(lst, cols):
+    return lst[:, cols.start // 16 : cols.stop // 16]
 
 
 def product(nc, out, words, scales, t, rhs, rhs_scale):
@@ -68,160 +68,202 @@ def tile_picked_laplace8_none_po_kernel(
         n2_t = lists.tile([P, S // 16], U16, name="n2_t")
         n3_t = lists.tile([P, S // 16], U16, name="n3_t")
 
-        xw = sb.tile([P, T], I32, name="xw", align_bytes=64)
-        xs = sb.tile([P, T], U8, name="xs", align_bytes=64)
+        xw = sb.tile([P, T], I32, name="xw", tag="xw", align_bytes=64)
+        xs = sb.tile([P, T], U8, name="xs", tag="xs", align_bytes=64)
         w1w = sb.tile([P, H], I32, name="w1w", tag="wraw", align_bytes=64)
         ws = sb.tile([P, H], U8, name="ws", align_bytes=64)
-        gain = sb.tile([P, PACK], F32, name="gain")
+
 
         nc.vector.memset(xs[:].bitcast(I32), 0)
-        nc.gpsimd.memset(ws[:].bitcast(I32), 0)
+        nc.vector.memset(ws[:].bitcast(I32), 0)
 
-        load_scale_rows([nc.scalar] * 4, xs, x_scales)
-        load_scale_rows([nc.scalar, nc.scalar, nc.scalar, nc.gpsimd], ws, w1_scales)
+        load_scale_rows([nc.sync] * 4, xs, x_scales)
         nc.sync.dma_start(offs_t[:], offs)
         nc.sync.dma_start(n1_t[:], n1)
-        nc.sync.dma_start(n2_t[:], n2)
-        nc.sync.dma_start(n3_t[:], n3)
         nc.sync.dma_start(out=w1w[:], in_=w1_words[0].rearrange("p n t -> p (n t)").bitcast(I32))
+        nc.sync.dma_start(n2_t[:], n2)
+        load_scale_rows([nc.sync] * 4, ws, w1_scales)
         nc.sync.dma_start(out=xw[:], in_=x_words[0].rearrange("p n t -> p (n t)").bitcast(I32))
-        nc.gpsimd.dma_start(out=gain[:], in_=gn.rearrange("(p t) o -> p (t o)", t=PACK))
+        nc.sync.dma_start(n3_t[:], n3)
+        w2w = sb.tile([P, N], I32, name="w2w", align_bytes=64)
+        nc.sync.dma_start(out=w2w[:], in_=w2_words[0].rearrange("p n t -> p (n t)").bitcast(I32))
 
         w1d = sb.tile([P, H], I32, name="w1d", align_bytes=64)
         w1sd = sb.tile([P, H], U8, name="w1sd", align_bytes=64)
         deal(nc, w1d[:], w1w[:], 4)
-        w2w = sb.tile([P, N], I32, name="w2w", tag="wraw", align_bytes=64)
-        nc.sync.dma_start(out=w2w[:], in_=w2_words[0].rearrange("p n t -> p (n t)").bitcast(I32))
         xsg = sb.tile([P, S], U8, name="xsg", align_bytes=64)
         nc.vector.tensor_copy(xsg[:], xs[:].indirect(offs_t[:]))
+        gain = sb.tile([P, PACK], F32, name="gain", tag="xs", align_bytes=64)
+        nc.sync.dma_start(out=gain[:], in_=gn.rearrange("(p t) o -> p (t o)", t=PACK))
         deal(nc, w1sd[:], ws[:], 16)
         load_scale_rows([nc.sync] * 4, ws, w2_scales)
 
         y = [sb.tile([P, S], F32, name="y%d" % t) for t in range(PACK)]
         acc1 = {}
+        xg = [sb.tile([P, HALF], U32, name="xg%d" % c, align_bytes=64) for c in range(2)]
         for c in range(2):
-            xg = sb.tile([P, HALF], U32, name="xg%d" % c, align_bytes=64)
-            nc.vector.tensor_copy(xg[:], xw[:].bitcast(U32).indirect(entries(offs_t, c)))
-            for t in range(PACK):
+            nc.vector.tensor_copy(xg[c][:], xw[:].bitcast(U32).indirect(entries(offs_t, half(c))))
+        for t0 in (0, 2):
+            for c, t in ((0, t0), (0, t0 + 1), (1, t0 + 1), (1, t0)):
                 acc1[c, t] = psum.tile([P, BANK], F32, name="acc", tag="bank%d" % (PACK * c + t))
-                product(nc, acc1[c, t][:, :HALF], w1d, w1sd, t, xg[:], xsg[:, half(c)])
-        for t in range(PACK):
-            for c in range(2):
+                product(nc, acc1[c, t][:, :HALF], w1d, w1sd, t, xg[c][:], xsg[:, half(c)])
                 nc.scalar.activation(y[t][:, half(c)], acc1[c, t][:, :HALF], ACT.Copy)
 
-        w2d = sb.tile([P, N], I32, name="w2d", align_bytes=64)
+        w2d = sb.tile([P, N], I32, name="w2d", tag="xw", align_bytes=64)
         w2sd = sb.tile([P, N], U8, name="w2sd", align_bytes=64)
         deal(nc, w2d[:], w2w[:], 4)
 
         diff = [sb.tile([P, PACK, HALF], F32, name="diff%d" % c) for c in range(2)]
-        size = [sb.tile([P, PACK, HALF], F32, name="size%d" % c, tag="size%d" % c) for c in range(2)]
         decay = [sb.tile([P, PACK, HALF], F32, name="decay%d" % c, tag="decay%d" % c, align_bytes=64) for c in range(2)]
-        hs = [sb.tile([P, PACK, HALF], F32, name="hs%d" % c) for c in range(2)]
         sq = [sb.tile([P, PACK, HALF], F32, name="sq%d" % c) for c in range(2)]
+        size = {}
         first = {}
-        zb = {}
         acc2 = {}
+        whole = slice(0, HALF)
+        quarters = (slice(0, HALF // 2), slice(HALF // 2, HALF))
 
-        def fetch_first(c, t, tag):
-            first[c, t] = sb.tile([P, HALF], F32, name="first", tag=tag, align_bytes=64)
-            nc.vector.tensor_copy(first[c, t][:], y[t][:].indirect(entries(n1_t, c)))
+        def rows_tile(store, c, ts, tag):
+            rows = sb.tile([P, len(ts), HALF], F32, name="rows", tag=tag, align_bytes=64)
+            for i, t in enumerate(ts):
+                store[c, t] = rows[:, i, :]
 
-        def fetch_second(c, t):
-            nc.vector.tensor_tensor(diff[c][:, t, :], y[t][:].indirect(entries(n2_t, c)), first[c, t][:], ALU.subtract)
-            nc.scalar.activation(size[c][:, t, :], diff[c][:, t, :], ACT.Abs)
-            nc.scalar.activation(decay[c][:, t, :], size[c][:, t, :], ACT.Exp, scale=-1.0)
+        def placed(c, cols):
+            return slice(c * HALF + cols.start, c * HALF + cols.stop)
 
-        def apply_gain(c):
-            zb[c] = sb.tile([P, HALF, PACK], BF16, name="zb", tag="zb%d" % c, align_bytes=64)
+        def fetch_first(c, t, cols):
+            nc.vector.tensor_copy(first[c, t][:, cols], y[t][:].indirect(entries(n1_t, placed(c, cols))))
+
+        def fetch_second(c, t, cols):
             nc.vector.tensor_tensor(
-                zb[c][:].rearrange("p (c i) t -> p c t i", i=4),
-                decay[c][:].rearrange("p t (c i) -> p c t i", i=4),
-                gain[:].unsqueeze(1).unsqueeze(3).broadcast_to([P, HALF // 4, PACK, 4]),
-                ALU.mult,
+                diff[c][:, t, cols], y[t][:].indirect(entries(n2_t, placed(c, cols))), first[c, t][:, cols], ALU.subtract
             )
 
-        def second_product(c):
-            zw = sb.tile([P, HALF], U32, name="zw%d" % c, align_bytes=64)
-            zs = sb.tile([P, HALF], U8, name="zs%d" % c, align_bytes=64)
-            nc.vector.quantize_mx(out=zw[:].bitcast(FP8X4), scales=zs[:], in_=zb[c][:].rearrange("p j t -> p (j t)"))
+        def take_size(c, t, cols):
+            nc.scalar.activation(size[c, t][:, cols], diff[c][:, t, cols], ACT.Abs)
+
+        def take_decay(c, t, cols):
+            nc.scalar.activation(decay[c][:, t, cols], size[c, t][:, cols], ACT.Exp, scale=-1.0)
+
+        def interleaved(tile):
+            return tile.rearrange("p (c i) t -> p c t i", i=4)
+
+        def second_product(c, cols, zb, name):
+            width = cols.stop - cols.start
+            zw = sb.tile([P, width], U32, name="zw" + name, align_bytes=64)
+            zs = sb.tile([P, width], U8, name="zs" + name, align_bytes=64)
+            nc.vector.quantize_mx(out=zw[:].bitcast(FP8X4), scales=zs[:], in_=zb[:].rearrange("p j t -> p (j t)"))
+            for t in range(PACK):
+                product(nc, acc2[c, t][:, cols], w2d, w2sd, t, zw[:], zs[:])
+
+        def square_h(c, t, cols):
+            nc.scalar.activation(sq[c][:, t, cols], acc2[c, t][:, cols], ACT.Square)
+
+
+        for c in range(2):
             for t in range(PACK):
                 acc2[c, t] = psum.tile([P, BANK], F32, name="acc", tag="bank%d" % (PACK * c + t))
-                product(nc, acc2[c, t][:, :HALF], w2d, w2sd, t, zw[:], zs[:])
-
-        def square_h(c, t):
-            nc.scalar.activation(sq[c][:, t, :], acc2[c, t][:, :HALF], ACT.Square)
-
-        def keep_h(c, t):
-            nc.vector.tensor_copy(hs[c][:, t, :], acc2[c, t][:, :HALF])
-
-        fetch_first(0, 0, "first00")
-        for t in range(PACK):
-            if t + 1 < PACK:
-                fetch_first(0, t + 1, "first0%d" % (t + 1))
-            else:
-                fetch_first(1, 0, "first10")
-            fetch_second(0, t)
-        fetch_second(1, 0)
+        rows_tile(first, 0, (0, 1), "first01")
+        rows_tile(first, 0, (2, 3), "first23")
+        rows_tile(size, 0, range(PACK), "size0")
+        z_planes = sb.tile([P, PACK, HALF], BF16, name="z_planes", tag="size1", align_bytes=64)
+        for pair in ((1, 0), (2, 3)):
+            for step in (fetch_first, fetch_second, take_size, take_decay):
+                for t in pair:
+                    step(0, t, whole)
+            for t in pair:
+                nc.scalar.activation(z_planes[:, t, :], decay[0][:, t, :], ACT.Copy, scale=gain[:, t : t + 1])
+        zb0 = sb.tile([P, HALF, PACK], BF16, name="zb0", tag="zb0", align_bytes=64)
+        nc.scalar.copy(interleaved(zb0[:]), z_planes[:].rearrange("p t (c i) -> p c t i", i=4))
+        rows_tile(size, 1, range(PACK), "size1")
+        rows_tile(first, 1, range(PACK - 1), "first23")
+        for step in (fetch_first, fetch_second, take_size, take_decay):
+            for t in range(PACK - 1):
+                step(1, t, whole)
         deal(nc, w2sd[:], ws[:], 16)
-        apply_gain(0)
-        fetch_first(1, 1, "decay0")
-        second_product(0)
-        fetch_first(1, 2, "zb0")
-        fetch_second(1, 1)
-        for t in range(PACK):
-            square_h(0, t)
-        fetch_first(1, 3, "decay0")
-        fetch_second(1, 2)
-        fetch_second(1, 3)
-        apply_gain(1)
-        second_product(1)
-        for t in range(PACK):
-            keep_h(0, t)
+        second_product(0, whole, zb0, "0")
+        rows_tile(first, 1, [PACK - 1], "zb0")
+        square_h(0, 0, whole)
+        square_h(0, 1, whole)
+        for step in (fetch_first, fetch_second, take_size, take_decay):
+            for cols in quarters:
+                step(1, PACK - 1, cols)
+        zb1 = sb.tile([P, HALF, PACK], BF16, name="zb1", align_bytes=64)
+        early = PACK - 1
+        nc.vector.tensor_tensor(
+            interleaved(zb1[:, :, :early]),
+            decay[1][:, :early, :].rearrange("p t (c i) -> p c t i", i=4),
+            gain[:, :early].unsqueeze(1).unsqueeze(3).broadcast_to([P, HALF // 4, early, 4]),
+            ALU.mult,
+        )
+        for cols in quarters:
+            nc.vector.tensor_scalar(zb1[:, cols, early], decay[1][:, early, cols], gain[:, early:], None, ALU.mult)
+        second_product(1, whole, zb1, "1")
+        hrow = [sb.tile([P, S], F32, name="hrow%d" % t, tag="decay1" if t == 2 else "hrow%d" % t, align_bytes=64) for t in range(PACK)]
+        for t in range(PACK - 1):
+            nc.vector.tensor_copy(hrow[t][:, half(0)], acc2[0, t][:, :HALF])
 
-        g = [sb.tile([P, S], F32, name="g%d" % t) for t in range(PACK)]
-        root = [sb.tile([P, PACK, HALF], F32, name="root%d" % c, tag="size%d" % (1 - c)) for c in range(2)]
-        inv = [sb.tile([P, PACK, HALF], F32, name="inv%d" % c) for c in range(2)]
+        ratio = [sb.tile([P, 2 * S], F32, name="ratio%d" % t) for t in range(PACK)]
+        root = [sb.tile([P, PACK, HALF], F32, name="root%d" % c, tag="size%d" % (1 - c), align_bytes=64) for c in range(2)]
+
+        def inv(t, cols):
+            return ratio[t][:, S + cols.start : S + cols.stop]
+
+        def take_root(c, t, cols):
+            nc.scalar.activation(root[c][:, t, cols], sq[c][:, t, cols], ACT.Abs_reciprocal_sqrt, bias=0.5)
+
+        def take_inverse(c, t, cols):
+            nc.scalar.activation(inv(t, placed(c, cols)), root[c][:, t, cols], ACT.Square)
+
+        def take_ratio(c, t, cols):
+            nc.vector.tensor_tensor(ratio[t][:, placed(c, cols)], hrow[t][:, placed(c, cols)], inv(t, placed(c, cols)), ALU.mult)
+
         for t in range(PACK):
-            keep_h(1, t)
-            square_h(1, t)
-            for c in (1, 0):
-                nc.scalar.activation(root[c][:, t, :], sq[c][:, t, :], ACT.Abs_reciprocal_sqrt, bias=0.5)
-                nc.scalar.activation(inv[c][:, t, :], root[c][:, t, :], ACT.Square)
-                nc.vector.tensor_tensor(g[t][:, half(c)], inv[c][:, t, :], hs[c][:, t, :], ALU.mult)
+            pieces = quarters if t == 0 else (whole,)
+            if t >= 2:
+                square_h(0, t, whole)
+            for cols in pieces:
+                square_h(1, t, cols)
+            if t < PACK - 1:
+                nc.vector.tensor_copy(hrow[t][:, half(1)], acc2[1, t][:, :HALF])
+            else:
+                for c in range(2):
+                    nc.scalar.activation(hrow[t][:, half(c)], acc2[c, t][:, :HALF], ACT.Copy)
+            for step in (take_root, take_inverse, take_ratio):
+                for cols in pieces:
+                    step(1, t, cols)
+            for step in (take_root, take_inverse, take_ratio):
+                step(0, t, whole)
 
         out_rows = out_0.rearrange("(p t) j -> p t j", t=PACK)
         out_words = out_1[0].rearrange("p n t -> p (n t)").bitcast(I32)
         ow = sb.tile([P, S], U32, name="ow", align_bytes=64)
         osc = sb.tile([P, S], U8, name="osc", align_bytes=64)
-        res = [sb.tile([P, PACK, HALF], F32, name="res%d" % c) for c in range(2)]
+        res = [sb.tile([P, 2, S], F32, name="res%d" % u) for u in range(2)]
 
-        def fetch_third(c, t):
-            nc.vector.tensor_tensor(res[c][:, t, :], g[t][:].indirect(entries(n3_t, c)), hs[c][:, t, :], ALU.mult)
+        def fetch_third(t, cols):
+            nc.vector.tensor_tensor(res[t // 2][:, t % 2, cols], ratio[t][:].indirect(entries(n3_t, cols)), hrow[t][:, cols], ALU.mult)
+            nc.sync.dma_start(out=out_rows[:, t, cols], in_=res[t // 2][:, t % 2, cols])
 
-        def store_rows(c, t0, t1):
-            nc.sync.dma_start(out=out_rows[:, t0:t1, half(c)], in_=res[c][:, t0:t1, :])
+        ob = [sb.tile([P, HALF, PACK], BF16, name="ob%d" % c, align_bytes=64) for c in range(2)]
 
-        def planes(c, copy):
-            ob = sb.tile([P, HALF, PACK], BF16, name="ob%d" % c, align_bytes=64)
-            copy(ob[:].rearrange("p (c i) t -> p c t i", i=4), res[c][:].rearrange("p t (c i) -> p c t i", i=4))
+        def round_rows(c, u, copy):
+            copy(interleaved(ob[c][:, :, 2 * u : 2 * u + 2]), res[u][:, :, half(c)].rearrange("p t (c i) -> p c t i", i=4))
+
+        def planes(c):
             nc.vector.quantize_mx(
-                out=ow[:, half(c)].bitcast(FP8X4), scales=osc[:, half(c)], in_=ob[:].rearrange("p j t -> p (j t)")
+                out=ow[:, half(c)].bitcast(FP8X4), scales=osc[:, half(c)], in_=ob[c][:].rearrange("p j t -> p (j t)")
             )
             nc.sync.dma_start(out=out_words[:, half(c)], in_=ow[:, half(c)].bitcast(I32))
 
-        for t in range(2):
-            for c in range(2):
-                fetch_third(c, t)
+        for t in range(PACK - 1):
+            fetch_third(t, slice(0, S))
         for c in range(2):
-            store_rows(c, 0, 2)
-        fetch_third(0, 2)
-        fetch_third(0, 3)
-        store_rows(0, 2, 4)
-        fetch_third(1, 2)
-        store_rows(1, 2, 3)
-        fetch_third(1, 3)
-        store_rows(1, 3, 4)
-        planes(1, nc.vector.tensor_copy)
-        planes(0, nc.scalar.copy)
+            fetch_third(PACK - 1, half(c))
+        for u, copy in ((0, nc.scalar.copy), (1, nc.vector.tensor_copy)):
+            for c in range(2):
+                round_rows(c, u, copy)
+        planes(0)
+        planes(1)
         for q in range(4):
-            nc.scalar.dma_start(out=out_2[0, 4 * q : 4 * q + 4, :].bitcast(I32), in_=osc[32 * q : 32 * q + 4, :].bitcast(I32))
+            queue = nc.sync if q == 0 else nc.scalar
+            queue.dma_start(out=out_2[0, 4 * q : 4 * q + 4, :].bitcast(I32), in_=osc[32 * q : 32 * q + 4, :].bitcast(I32))

from contextlib import ExitStack

import concourse.mybir as mybir

K, T, S, H, N = 512, 2048, 512, 512, 512
FLOPS = 2 * K * H * S + 2 * H * N * S

F32 = mybir.dt.float32
BF16 = mybir.dt.bfloat16
I32 = mybir.dt.int32
U32 = mybir.dt.uint32
U16 = mybir.dt.uint16
U8 = mybir.dt.uint8
FP8X4 = mybir.dt.float8_e4m3fn_x4
ACT = mybir.ActivationFunctionType
ALU = mybir.AluOpType

P = 128
PACK = 4
BANK = 512
HALF = S // 2


def half(c):
    return slice(c * HALF, (c + 1) * HALF)


def entries(lst, cols):
    return lst[:, cols.start // 16 : cols.stop // 16]


def product(nc, out, words, scales, t, rhs, rhs_scale):
    cols = slice(t * P, (t + 1) * P)
    nc.tensor.matmul_mx(
        out=out,
        lhsT=words[:, cols].bitcast(FP8X4),
        lhsT_scale=scales[:, cols],
        rhs=rhs.bitcast(FP8X4),
        rhs_scale=rhs_scale,
        start=True,
        stop=True,
    )


def load_scale_rows(queues, plane, scales):
    for q, queue in enumerate(queues):
        queue.dma_start(out=plane[32 * q : 32 * q + 4, :].bitcast(I32), in_=scales[0, 4 * q : 4 * q + 4, :].bitcast(I32))


def deal(nc, out, in_, run):
    nc.vector.tensor_copy(
        out=out.rearrange("p (t c i) -> p c t i", t=PACK, i=run),
        in_=in_.rearrange("p (c i t) -> p c t i", t=PACK, i=run),
    )


def tile_picked_laplace8_none_po_kernel(
    tc, x_words, x_scales, w1_words, w1_scales, gn, w2_words, w2_scales, offs, n1, n2, n3, out_0, out_1, out_2
):
    nc = tc.nc
    with ExitStack() as ctx:
        lists = ctx.enter_context(tc.tile_pool(name="lists", bufs=1))
        sb = ctx.enter_context(tc.tile_pool(name="sb", bufs=1))
        psum = ctx.enter_context(tc.psum_pool(name="psum", bufs=1))

        offs_t = lists.tile([P, S // 16], U16, name="offs_t")
        n1_t = lists.tile([P, S // 16], U16, name="n1_t")
        n2_t = lists.tile([P, S // 16], U16, name="n2_t")
        n3_t = lists.tile([P, S // 16], U16, name="n3_t")

        xw = sb.tile([P, T], I32, name="xw", tag="xw", align_bytes=64)
        xs = sb.tile([P, T], U8, name="xs", tag="xs", align_bytes=64)
        w1w = sb.tile([P, H], I32, name="w1w", tag="wraw", align_bytes=64)
        ws = sb.tile([P, H], U8, name="ws", align_bytes=64)


        nc.vector.memset(xs[:].bitcast(I32), 0)
        nc.vector.memset(ws[:].bitcast(I32), 0)

        load_scale_rows([nc.sync] * 4, xs, x_scales)
        nc.sync.dma_start(offs_t[:], offs)
        nc.sync.dma_start(n1_t[:], n1)
        nc.sync.dma_start(out=w1w[:], in_=w1_words[0].rearrange("p n t -> p (n t)").bitcast(I32))
        nc.sync.dma_start(n2_t[:], n2)
        load_scale_rows([nc.sync] * 4, ws, w1_scales)
        nc.sync.dma_start(out=xw[:], in_=x_words[0].rearrange("p n t -> p (n t)").bitcast(I32))
        nc.sync.dma_start(n3_t[:], n3)
        w2w = sb.tile([P, N], I32, name="w2w", align_bytes=64)
        nc.sync.dma_start(out=w2w[:], in_=w2_words[0].rearrange("p n t -> p (n t)").bitcast(I32))

        w1d = sb.tile([P, H], I32, name="w1d", align_bytes=64)
        w1sd = sb.tile([P, H], U8, name="w1sd", align_bytes=64)
        deal(nc, w1d[:], w1w[:], 4)
        xsg = sb.tile([P, S], U8, name="xsg", align_bytes=64)
        nc.vector.tensor_copy(xsg[:], xs[:].indirect(offs_t[:]))
        gain = sb.tile([P, PACK], F32, name="gain", tag="xs", align_bytes=64)
        nc.sync.dma_start(out=gain[:], in_=gn.rearrange("(p t) o -> p (t o)", t=PACK))
        deal(nc, w1sd[:], ws[:], 16)
        load_scale_rows([nc.sync] * 4, ws, w2_scales)

        y = [sb.tile([P, S], F32, name="y%d" % t) for t in range(PACK)]
        acc1 = {}
        xg = [sb.tile([P, HALF], U32, name="xg%d" % c, align_bytes=64) for c in range(2)]
        for c in range(2):
            nc.vector.tensor_copy(xg[c][:], xw[:].bitcast(U32).indirect(entries(offs_t, half(c))))
        for t0 in (0, 2):
            for c, t in ((0, t0), (0, t0 + 1), (1, t0 + 1), (1, t0)):
                acc1[c, t] = psum.tile([P, BANK], F32, name="acc", tag="bank%d" % (PACK * c + t))
                product(nc, acc1[c, t][:, :HALF], w1d, w1sd, t, xg[c][:], xsg[:, half(c)])
                nc.scalar.activation(y[t][:, half(c)], acc1[c, t][:, :HALF], ACT.Copy)

        w2d = sb.tile([P, N], I32, name="w2d", tag="xw", align_bytes=64)
        w2sd = sb.tile([P, N], U8, name="w2sd", align_bytes=64)
        deal(nc, w2d[:], w2w[:], 4)

        diff = [sb.tile([P, PACK, HALF], F32, name="diff%d" % c) for c in range(2)]
        decay = [sb.tile([P, PACK, HALF], F32, name="decay%d" % c, tag="decay%d" % c, align_bytes=64) for c in range(2)]
        sq = [sb.tile([P, PACK, HALF], F32, name="sq%d" % c) for c in range(2)]
        size = {}
        first = {}
        acc2 = {}
        whole = slice(0, HALF)
        quarters = (slice(0, HALF // 2), slice(HALF // 2, HALF))

        def rows_tile(store, c, ts, tag):
            rows = sb.tile([P, len(ts), HALF], F32, name="rows", tag=tag, align_bytes=64)
            for i, t in enumerate(ts):
                store[c, t] = rows[:, i, :]

        def placed(c, cols):
            return slice(c * HALF + cols.start, c * HALF + cols.stop)

        def fetch_first(c, t, cols):
            nc.vector.tensor_copy(first[c, t][:, cols], y[t][:].indirect(entries(n1_t, placed(c, cols))))

        def fetch_second(c, t, cols):
            nc.vector.tensor_tensor(
                diff[c][:, t, cols], y[t][:].indirect(entries(n2_t, placed(c, cols))), first[c, t][:, cols], ALU.subtract
            )

        def take_size(c, t, cols):
            nc.scalar.activation(size[c, t][:, cols], diff[c][:, t, cols], ACT.Abs)

        def take_decay(c, t, cols):
            nc.scalar.activation(decay[c][:, t, cols], size[c, t][:, cols], ACT.Exp, scale=-1.0)

        def interleaved(tile):
            return tile.rearrange("p (c i) t -> p c t i", i=4)

        def second_product(c, cols, zb, name):
            width = cols.stop - cols.start
            zw = sb.tile([P, width], U32, name="zw" + name, align_bytes=64)
            zs = sb.tile([P, width], U8, name="zs" + name, align_bytes=64)
            nc.vector.quantize_mx(out=zw[:].bitcast(FP8X4), scales=zs[:], in_=zb[:].rearrange("p j t -> p (j t)"))
            for t in range(PACK):
                product(nc, acc2[c, t][:, cols], w2d, w2sd, t, zw[:], zs[:])

        def square_h(c, t, cols):
            nc.scalar.activation(sq[c][:, t, cols], acc2[c, t][:, cols], ACT.Square)


        for c in range(2):
            for t in range(PACK):
                acc2[c, t] = psum.tile([P, BANK], F32, name="acc", tag="bank%d" % (PACK * c + t))
        rows_tile(first, 0, (0, 1), "first01")
        rows_tile(first, 0, (2, 3), "first23")
        rows_tile(size, 0, range(PACK), "size0")
        z_planes = sb.tile([P, PACK, HALF], BF16, name="z_planes", tag="size1", align_bytes=64)
        for pair in ((1, 0), (2, 3)):
            for step in (fetch_first, fetch_second, take_size, take_decay):
                for t in pair:
                    step(0, t, whole)
            for t in pair:
                nc.scalar.activation(z_planes[:, t, :], decay[0][:, t, :], ACT.Copy, scale=gain[:, t : t + 1])
        zb0 = sb.tile([P, HALF, PACK], BF16, name="zb0", tag="zb0", align_bytes=64)
        nc.scalar.copy(interleaved(zb0[:]), z_planes[:].rearrange("p t (c i) -> p c t i", i=4))
        rows_tile(size, 1, range(PACK), "size1")
        rows_tile(first, 1, range(PACK - 1), "first23")
        for step in (fetch_first, fetch_second, take_size, take_decay):
            for t in range(PACK - 1):
                step(1, t, whole)
        deal(nc, w2sd[:], ws[:], 16)
        second_product(0, whole, zb0, "0")
        rows_tile(first, 1, [PACK - 1], "zb0")
        square_h(0, 0, whole)
        square_h(0, 1, whole)
        for step in (fetch_first, fetch_second, take_size, take_decay):
            for cols in quarters:
                step(1, PACK - 1, cols)
        zb1 = sb.tile([P, HALF, PACK], BF16, name="zb1", align_bytes=64)
        early = PACK - 1
        nc.vector.tensor_tensor(
            interleaved(zb1[:, :, :early]),
            decay[1][:, :early, :].rearrange("p t (c i) -> p c t i", i=4),
            gain[:, :early].unsqueeze(1).unsqueeze(3).broadcast_to([P, HALF // 4, early, 4]),
            ALU.mult,
        )
        for cols in quarters:
            nc.vector.tensor_scalar(zb1[:, cols, early], decay[1][:, early, cols], gain[:, early:], None, ALU.mult)
        second_product(1, whole, zb1, "1")
        hrow = [sb.tile([P, S], F32, name="hrow%d" % t, tag="decay1" if t == 2 else "hrow%d" % t, align_bytes=64) for t in range(PACK)]
        for t in range(PACK - 1):
            nc.vector.tensor_copy(hrow[t][:, half(0)], acc2[0, t][:, :HALF])

        ratio = [sb.tile([P, 2 * S], F32, name="ratio%d" % t) for t in range(PACK)]
        root = [sb.tile([P, PACK, HALF], F32, name="root%d" % c, tag="size%d" % (1 - c), align_bytes=64) for c in range(2)]

        def inv(t, cols):
            return ratio[t][:, S + cols.start : S + cols.stop]

        def take_root(c, t, cols):
            nc.scalar.activation(root[c][:, t, cols], sq[c][:, t, cols], ACT.Abs_reciprocal_sqrt, bias=0.5)

        def take_inverse(c, t, cols):
            nc.scalar.activation(inv(t, placed(c, cols)), root[c][:, t, cols], ACT.Square)

        def take_ratio(c, t, cols):
            nc.vector.tensor_tensor(ratio[t][:, placed(c, cols)], hrow[t][:, placed(c, cols)], inv(t, placed(c, cols)), ALU.mult)

        for t in range(PACK):
            pieces = quarters if t == 0 else (whole,)
            if t >= 2:
                square_h(0, t, whole)
            for cols in pieces:
                square_h(1, t, cols)
            if t < PACK - 1:
                nc.vector.tensor_copy(hrow[t][:, half(1)], acc2[1, t][:, :HALF])
            else:
                for c in range(2):
                    nc.scalar.activation(hrow[t][:, half(c)], acc2[c, t][:, :HALF], ACT.Copy)
            for step in (take_root, take_inverse, take_ratio):
                for cols in pieces:
                    step(1, t, cols)
            for step in (take_root, take_inverse, take_ratio):
                step(0, t, whole)

        out_rows = out_0.rearrange("(p t) j -> p t j", t=PACK)
        out_words = out_1[0].rearrange("p n t -> p (n t)").bitcast(I32)
        ow = sb.tile([P, S], U32, name="ow", align_bytes=64)
        osc = sb.tile([P, S], U8, name="osc", align_bytes=64)
        res = [sb.tile([P, 2, S], F32, name="res%d" % u) for u in range(2)]

        def fetch_third(t, cols):
            nc.vector.tensor_tensor(res[t // 2][:, t % 2, cols], ratio[t][:].indirect(entries(n3_t, cols)), hrow[t][:, cols], ALU.mult)
            nc.sync.dma_start(out=out_rows[:, t, cols], in_=res[t // 2][:, t % 2, cols])

        ob = [sb.tile([P, HALF, PACK], BF16, name="ob%d" % c, align_bytes=64) for c in range(2)]

        def round_rows(c, u, copy):
            copy(interleaved(ob[c][:, :, 2 * u : 2 * u + 2]), res[u][:, :, half(c)].rearrange("p t (c i) -> p c t i", i=4))

        def planes(c):
            nc.vector.quantize_mx(
                out=ow[:, half(c)].bitcast(FP8X4), scales=osc[:, half(c)], in_=ob[c][:].rearrange("p j t -> p (j t)")
            )
            nc.sync.dma_start(out=out_words[:, half(c)], in_=ow[:, half(c)].bitcast(I32))

        for t in range(PACK - 1):
            fetch_third(t, slice(0, S))
        for c in range(2):
            fetch_third(PACK - 1, half(c))
        for u, copy in ((0, nc.scalar.copy), (1, nc.vector.tensor_copy)):
            for c in range(2):
                round_rows(c, u, copy)
        planes(0)
        planes(1)
        for q in range(4):
            queue = nc.sync if q == 0 else nc.scalar
            queue.dma_start(out=out_2[0, 4 * q : 4 * q + 4, :].bitcast(I32), in_=osc[32 * q : 32 * q + 4, :].bitcast(I32))
